import numpy as np
import ml_dtypes

BF16 = ml_dtypes.bfloat16


def bf(x):
    return np.asarray(x, np.float32).astype(BF16)


def f32(x):
    return np.asarray(x, np.float32)


def f64(x):
    return np.asarray(x).astype(np.float64)


def striped(idx):
    return np.concatenate([l.reshape(-1, 16).T for l in idx])


def rows(idx, k):
    return np.tile(np.repeat(idx, 16, axis=0), (k // (16 * 8), 1))


def look(tab, idx):
    return np.take_along_axis(f64(tab), rows(idx, len(tab)), axis=1)


P, K, S, R, V, N = 128, 128, 2048, 1, 1024, 1024


def setup_inputs():
    return {"tab": f32(np.random.standard_normal((2, K, S))), "q": f32(0.5 * np.random.standard_normal((K, 1))), "e": bf(np.repeat(np.eye(8), 16, axis=0)), "et": bf(np.repeat(np.eye(8), 16, axis=0).T), "sk": f32(8.0 + np.random.standard_normal((8 * R, 1))), "offs": striped(np.stack([np.random.permutation(S)[:N] for _ in range(8)]))}


def reference(tab, q, e, et, sk, offs):
    idx = np.stack([g.T.reshape(-1) for g in np.split(offs, 8)])
    k = f64(q) * look(tab[0], idx)
    s = np.concatenate([f64(e).T @ k[a:a + P] for a in range(0, K, P)])
    p = np.exp(s)
    p = p / (np.exp(f64(sk)) + p.sum(axis=1, keepdims=True))
    p = np.concatenate([f64(et).T @ p[a:a + 8] for a in range(0, len(p), 8)])
    x = (p * look(tab[1], idx)).sum(axis=1).reshape(-1, P)
    return x

@@ -1,0 +1,104 @@
+import concourse.mybir as mybir
+
+P = 128
+HEADS = 8
+HEAD_ROWS = P // HEADS
+PLACES = 2048
+N = 1024
+PIECE = 512
+PIECES = N // PIECE
+BLOCK = 32
+
+FLOPS = 4 * P * N
+
+F32, BF16, U16 = mybir.dt.float32, mybir.dt.bfloat16, mybir.dt.uint16
+ALU = mybir.AluOpType
+ACT = mybir.ActivationFunctionType
+
+
+def tile_lookup_hattn_sink_out_kernel(tc, tab, q, e, et, sk, offs, out):
+    nc = tc.nc
+    with (
+        tc.tile_pool(name="held", bufs=1) as held,
+        tc.tile_pool(name="work", bufs=PIECES) as work,
+        tc.psum_pool(name="psum", bufs=PIECES) as psum,
+    ):
+        offsets = held.tile([P, N // 16], U16)
+        keys = held.tile([P, PLACES], F32)
+        values = held.tile([P, PLACES], F32)
+        nc.sync.dma_start(offsets[:], offs)
+        nc.sync.dma_start(keys[:], tab[0])
+        nc.sync.dma_start(values[:], tab[1])
+
+        q_col = held.tile([P, 1], F32)
+        head_of = held.tile([P, HEADS], BF16)
+        sinks = held.tile([P, HEADS], F32)
+        nc.scalar.dma_start(q_col[:], q)
+        nc.scalar.dma_start(head_of[:], e)
+        nc.scalar.dma_start(sinks[:], sk.rearrange("h o -> (h o)").partition_broadcast(P))
+
+        zero = held.tile([P, 1], F32)
+        nc.vector.memset(zero[:], 0.0)
+        sums = held.tile([P, 1 + PIECES], F32)
+        nc.vector.memset(sums[:, 0:1], 1.0)
+        result = held.tile([P, BLOCK], F32, align_bytes=64)
+        nc.vector.memset(result[:], 0.0)
+
+        same_head = held.tile([P, P], F32)
+        nc.vector.tensor_copy(
+            same_head[:].rearrange("p (h r) -> p h r", h=HEADS),
+            head_of[:].unsqueeze(2).to_broadcast([P, HEADS, HEAD_ROWS]),
+        )
+
+        neg_top = held.tile([P, 1 + PIECES], F32)
+        own_sink = held.tile([P, HEADS], F32)
+        nc.vector.scalar_tensor_tensor(
+            own_sink[:], sinks[:], -1.0, head_of[:], ALU.mult, ALU.mult, accum_out=neg_top[:, 0:1]
+        )
+
+        def entries(c):
+            return offsets[:, c * (PIECE // 16) : (c + 1) * (PIECE // 16)]
+
+        weights = []
+        for c in range(PIECES):
+            kq = work.tile([P, PIECE], F32)
+            nc.vector.tensor_scalar(kq[:], keys[:].indirect(entries(c)), q_col[:], zero[:], ALU.mult, ALU.add)
+            scores = psum.tile([P, PIECE], F32)
+            nc.tensor.matmul(scores[:], same_head[:], kq[:], start=True, stop=True)
+            neg_scores = work.tile([P, PIECE], F32)
+            nc.vector.tensor_scalar(
+                neg_scores[:], scores[:], -1.0, neg_top[:, c : c + 1], ALU.mult, ALU.min,
+                accum_out=neg_top[:, c + 1 : c + 2],
+            )
+            weight = work.tile([P, PIECE], F32)
+            nc.scalar.activation(
+                weight[:], neg_scores[:], ACT.Exp, bias=neg_top[:, c + 1 : c + 2], scale=-1.0,
+                accum_out=sums[:, c + 1 : c + 2],
+            )
+            weights.append(weight)
+
+        rescale = held.tile([P, 1 + PIECES], F32)
+        nc.scalar.activation(rescale[:], neg_top[:], ACT.Exp, bias=neg_top[:, PIECES : PIECES + 1], scale=-1.0)
+        terms = held.tile([P, 1 + PIECES], F32)
+        denom = held.tile([P, 1], F32)
+        nc.vector.scalar_tensor_tensor(terms[:], rescale[:], 1.0, sums[:], ALU.mult, ALU.mult, accum_out=denom[:])
+        inv_denom = held.tile([P, 1], F32)
+        nc.vector.reciprocal(inv_denom[:], denom[:])
+
+        partial = held.tile([P, PIECES], F32)
+        for c in range(PIECES):
+            pv = work.tile([P, PIECE], F32)
+            nc.vector.tensor_tensor(pv[:], values[:].indirect(entries(c)), weights[c][:], ALU.mult)
+            if c < PIECES - 1:
+                copied = work.tile([P, PIECE], BF16)
+                nc.scalar.activation(copied[:], pv[:], ACT.Copy, accum_out=partial[:, c : c + 1])
+            else:
+                nc.vector.tensor_reduce(partial[:, c : c + 1], pv[:], mybir.AxisListType.X, ALU.add)
+
+        scaled = held.tile([P, PIECES], F32)
+        nc.vector.scalar_tensor_tensor(
+            scaled[:], partial[:], inv_denom[:], rescale[:, 1:], ALU.mult, ALU.mult, accum_out=result[:, 0:1]
+        )
+        rows = held.tile([P, BLOCK], F32, align_bytes=64)
+        nc.vector.transpose(rows[:], result[:])
+        nc.sync.dma_start(out.rearrange("o (b j) -> (o b) j", j=BLOCK), rows[0:P:BLOCK, :])

@@ -5,8 +5,9 @@ HEADS = 8
 HEAD_ROWS = P // HEADS
 PLACES = 2048
 N = 1024
-PIECE = 512
+PIECE = 256
 PIECES = N // PIECE
+WARM_UPS = 12
 BLOCK = 32
 
 FLOPS = 4 * P * N
@@ -22,23 +23,28 @@ def tile_lookup_hattn_sink_out_kernel(tc, tab, q, e, et, sk, offs, out):
         tc.tile_pool(name="held", bufs=1) as held,
         tc.tile_pool(name="work", bufs=PIECES) as work,
         tc.psum_pool(name="psum", bufs=PIECES) as psum,
+        tc.psum_pool(name="warm", bufs=1) as warm,
     ):
         offsets = held.tile([P, N // 16], U16)
         keys = held.tile([P, PLACES], F32)
-        values = held.tile([P, PLACES], F32)
         nc.sync.dma_start(offsets[:], offs)
         nc.sync.dma_start(keys[:], tab[0])
-        nc.sync.dma_start(values[:], tab[1])
 
         q_col = held.tile([P, 1], F32)
         head_of = held.tile([P, HEADS], BF16)
-        sinks = held.tile([P, HEADS], F32)
+        sinks = held.tile([P, HEADS], F32, tag="sinks_then_values")
         nc.scalar.dma_start(q_col[:], q)
         nc.scalar.dma_start(head_of[:], e)
         nc.scalar.dma_start(sinks[:], sk.rearrange("h o -> (h o)").partition_broadcast(P))
 
-        zero = held.tile([P, 1], F32)
-        nc.vector.memset(zero[:], 0.0)
+        zeros = held.tile([P, 512], BF16)
+        nc.vector.memset(zeros[:], 0.0)
+        idle = warm.tile([P, 512], F32)
+        for w in range(WARM_UPS):
+            nc.tensor.matmul(idle[:], zeros[:, 0:P], zeros[:], start=True, stop=True)
+
+        q_rows = held.tile([P, PIECE], F32)
+        nc.vector.tensor_copy(q_rows[:], q_col[:].to_broadcast([P, PIECE]))
         sums = held.tile([P, 1 + PIECES], F32)
         nc.vector.memset(sums[:, 0:1], 1.0)
         result = held.tile([P, BLOCK], F32, align_bytes=64)
@@ -56,29 +62,30 @@ def tile_lookup_hattn_sink_out_kernel(tc, tab, q, e, et, sk, offs, out):
             own_sink[:], sinks[:], -1.0, head_of[:], ALU.mult, ALU.mult, accum_out=neg_top[:, 0:1]
         )
 
+        values = held.tile([P, PLACES], F32, tag="sinks_then_values")
+        nc.sync.dma_start(values[:], tab[1])
+
         def entries(c):
             return offsets[:, c * (PIECE // 16) : (c + 1) * (PIECE // 16)]
 
         weights = []
         for c in range(PIECES):
             kq = work.tile([P, PIECE], F32)
-            nc.vector.tensor_scalar(kq[:], keys[:].indirect(entries(c)), q_col[:], zero[:], ALU.mult, ALU.add)
+            nc.vector.tensor_tensor(kq[:], keys[:].indirect(entries(c)), q_rows[:], ALU.mult)
             scores = psum.tile([P, PIECE], F32)
             nc.tensor.matmul(scores[:], same_head[:], kq[:], start=True, stop=True)
-            neg_scores = work.tile([P, PIECE], F32)
-            nc.vector.tensor_scalar(
-                neg_scores[:], scores[:], -1.0, neg_top[:, c : c + 1], ALU.mult, ALU.min,
-                accum_out=neg_top[:, c + 1 : c + 2],
-            )
+            nc.vector.tensor_reduce(neg_top[:, c + 1 : c + 2], scores[:], mybir.AxisListType.X, ALU.max, negate=True)
             weight = work.tile([P, PIECE], F32)
             nc.scalar.activation(
-                weight[:], neg_scores[:], ACT.Exp, bias=neg_top[:, c + 1 : c + 2], scale=-1.0,
+                weight[:], scores[:], ACT.Exp, bias=neg_top[:, c + 1 : c + 2],
                 accum_out=sums[:, c + 1 : c + 2],
             )
             weights.append(weight)
 
+        neg_all = held.tile([P, 1], F32)
+        nc.vector.tensor_reduce(neg_all[:], neg_top[:], mybir.AxisListType.X, ALU.min)
         rescale = held.tile([P, 1 + PIECES], F32)
-        nc.scalar.activation(rescale[:], neg_top[:], ACT.Exp, bias=neg_top[:, PIECES : PIECES + 1], scale=-1.0)
+        nc.scalar.activation(rescale[:], neg_top[:], ACT.Exp, bias=neg_all[:], scale=-1.0)
         terms = held.tile([P, 1 + PIECES], F32)
         denom = held.tile([P, 1], F32)
         nc.vector.scalar_tensor_tensor(terms[:], rescale[:], 1.0, sums[:], ALU.mult, ALU.mult, accum_out=denom[:])

@@ -7,7 +7,6 @@ PLACES = 2048
 N = 1024
 PIECE = 256
 PIECES = N // PIECE
-WARM_UPS = 12
 BLOCK = 32
 
 FLOPS = 4 * P * N
@@ -23,25 +22,18 @@ def tile_lookup_hattn_sink_out_kernel(tc, tab, q, e, et, sk, offs, out):
         tc.tile_pool(name="held", bufs=1) as held,
         tc.tile_pool(name="work", bufs=PIECES) as work,
         tc.psum_pool(name="psum", bufs=PIECES) as psum,
-        tc.psum_pool(name="warm", bufs=1) as warm,
     ):
         offsets = held.tile([P, N // 16], U16)
         keys = held.tile([P, PLACES], F32)
-        nc.sync.dma_start(offsets[:], offs)
-        nc.sync.dma_start(keys[:], tab[0])
-
-        q_col = held.tile([P, 1], F32)
         head_of = held.tile([P, HEADS], BF16)
-        sinks = held.tile([P, HEADS], F32, tag="sinks_then_values")
-        nc.scalar.dma_start(q_col[:], q)
-        nc.scalar.dma_start(head_of[:], e)
-        nc.scalar.dma_start(sinks[:], sk.rearrange("h o -> (h o)").partition_broadcast(P))
+        nc.sync.dma_start(head_of[:], e)
+        nc.sync.dma_start(keys[:], tab[0])
+        nc.sync.dma_start(offsets[:], offs)
 
-        zeros = held.tile([P, 512], BF16)
-        nc.vector.memset(zeros[:], 0.0)
-        idle = warm.tile([P, 512], F32)
-        for w in range(WARM_UPS):
-            nc.tensor.matmul(idle[:], zeros[:, 0:P], zeros[:], start=True, stop=True)
+        q_col = held.tile([P, 1], F32, tag="q_then_values")
+        sinks = held.tile([P, HEADS], F32)
+        nc.scalar.dma_start(q_col[:], q)
+        nc.scalar.dma_start(sinks[:], sk.rearrange("h o -> (h o)").partition_broadcast(P))
 
         q_rows = held.tile([P, PIECE], F32)
         nc.vector.tensor_copy(q_rows[:], q_col[:].to_broadcast([P, PIECE]))
@@ -50,7 +42,7 @@ def tile_lookup_hattn_sink_out_kernel(tc, tab, q, e, et, sk, offs, out):
         result = held.tile([P, BLOCK], F32, align_bytes=64)
         nc.vector.memset(result[:], 0.0)
 
-        same_head = held.tile([P, P], F32)
+        same_head = held.tile([P, P], BF16)
         nc.vector.tensor_copy(
             same_head[:].rearrange("p (h r) -> p h r", h=HEADS),
             head_of[:].unsqueeze(2).to_broadcast([P, HEADS, HEAD_ROWS]),
@@ -62,7 +54,7 @@ def tile_lookup_hattn_sink_out_kernel(tc, tab, q, e, et, sk, offs, out):
             own_sink[:], sinks[:], -1.0, head_of[:], ALU.mult, ALU.mult, accum_out=neg_top[:, 0:1]
         )
 
-        values = held.tile([P, PLACES], F32, tag="sinks_then_values")
+        values = held.tile([P, PLACES], F32, tag="q_then_values")
         nc.sync.dma_start(values[:], tab[1])
 
         def entries(c):
@@ -72,9 +64,16 @@ def tile_lookup_hattn_sink_out_kernel(tc, tab, q, e, et, sk, offs, out):
         for c in range(PIECES):
             kq = work.tile([P, PIECE], F32)
             nc.vector.tensor_tensor(kq[:], keys[:].indirect(entries(c)), q_rows[:], ALU.mult)
+            kq_rounded = work.tile([P, PIECE], BF16)
+            nc.scalar.copy(kq_rounded[:], kq[:])
+            rough_scores = psum.tile([P, PIECE], BF16)
+            nc.tensor.matmul(rough_scores[:], same_head[:], kq_rounded[:], start=True, stop=True)
             scores = psum.tile([P, PIECE], F32)
-            nc.tensor.matmul(scores[:], same_head[:], kq[:], start=True, stop=True)
-            nc.vector.tensor_reduce(neg_top[:, c + 1 : c + 2], scores[:], mybir.AxisListType.X, ALU.max, negate=True)
+            nc.tensor.matmul(scores[:], same_head[:], kq_rounded[:], start=True, stop=True)
+            negated = work.tile([P, PIECE], BF16)
+            nc.vector.tensor_scalar(
+                negated[:], rough_scores[:], -1.0, None, ALU.mult, ALU.min, accum_out=neg_top[:, c + 1 : c + 2]
+            )
             weight = work.tile([P, PIECE], F32)
             nc.scalar.activation(
                 weight[:], scores[:], ACT.Exp, bias=neg_top[:, c + 1 : c + 2],

import concourse.mybir as mybir

P = 128
HEADS = 8
HEAD_ROWS = P // HEADS
PLACES = 2048
N = 1024
PIECE = 256
PIECES = N // PIECE
BLOCK = 32

FLOPS = 4 * P * N

F32, BF16, U16 = mybir.dt.float32, mybir.dt.bfloat16, mybir.dt.uint16
ALU = mybir.AluOpType
ACT = mybir.ActivationFunctionType


def tile_lookup_hattn_sink_out_kernel(tc, tab, q, e, et, sk, offs, out):
    nc = tc.nc
    with (
        tc.tile_pool(name="held", bufs=1) as held,
        tc.tile_pool(name="work", bufs=PIECES) as work,
        tc.psum_pool(name="psum", bufs=PIECES) as psum,
    ):
        offsets = held.tile([P, N // 16], U16)
        keys = held.tile([P, PLACES], F32)
        head_of = held.tile([P, HEADS], BF16)
        nc.sync.dma_start(head_of[:], e)
        nc.sync.dma_start(keys[:], tab[0])
        nc.sync.dma_start(offsets[:], offs)

        q_col = held.tile([P, 1], F32, tag="q_then_values")
        sinks = held.tile([P, HEADS], F32)
        nc.scalar.dma_start(q_col[:], q)
        nc.scalar.dma_start(sinks[:], sk.rearrange("h o -> (h o)").partition_broadcast(P))

        q_rows = held.tile([P, PIECE], F32)
        nc.vector.tensor_copy(q_rows[:], q_col[:].to_broadcast([P, PIECE]))
        sums = held.tile([P, 1 + PIECES], F32)
        nc.vector.memset(sums[:, 0:1], 1.0)
        result = held.tile([P, BLOCK], F32, align_bytes=64)
        nc.vector.memset(result[:], 0.0)

        same_head = held.tile([P, P], BF16)
        nc.vector.tensor_copy(
            same_head[:].rearrange("p (h r) -> p h r", h=HEADS),
            head_of[:].unsqueeze(2).to_broadcast([P, HEADS, HEAD_ROWS]),
        )

        neg_top = held.tile([P, 1 + PIECES], F32)
        own_sink = held.tile([P, HEADS], F32)
        nc.vector.scalar_tensor_tensor(
            own_sink[:], sinks[:], -1.0, head_of[:], ALU.mult, ALU.mult, accum_out=neg_top[:, 0:1]
        )

        values = held.tile([P, PLACES], F32, tag="q_then_values")
        nc.sync.dma_start(values[:], tab[1])

        def entries(c):
            return offsets[:, c * (PIECE // 16) : (c + 1) * (PIECE // 16)]

        weights = []
        for c in range(PIECES):
            kq = work.tile([P, PIECE], F32)
            nc.vector.tensor_tensor(kq[:], keys[:].indirect(entries(c)), q_rows[:], ALU.mult)
            kq_rounded = work.tile([P, PIECE], BF16)
            nc.scalar.copy(kq_rounded[:], kq[:])
            rough_scores = psum.tile([P, PIECE], BF16)
            nc.tensor.matmul(rough_scores[:], same_head[:], kq_rounded[:], start=True, stop=True)
            scores = psum.tile([P, PIECE], F32)
            nc.tensor.matmul(scores[:], same_head[:], kq_rounded[:], start=True, stop=True)
            negated = work.tile([P, PIECE], BF16)
            nc.vector.tensor_scalar(
                negated[:], rough_scores[:], -1.0, None, ALU.mult, ALU.min, accum_out=neg_top[:, c + 1 : c + 2]
            )
            weight = work.tile([P, PIECE], F32)
            nc.scalar.activation(
                weight[:], scores[:], ACT.Exp, bias=neg_top[:, c + 1 : c + 2],
                accum_out=sums[:, c + 1 : c + 2],
            )
            weights.append(weight)

        neg_all = held.tile([P, 1], F32)
        nc.vector.tensor_reduce(neg_all[:], neg_top[:], mybir.AxisListType.X, ALU.min)
        rescale = held.tile([P, 1 + PIECES], F32)
        nc.scalar.activation(rescale[:], neg_top[:], ACT.Exp, bias=neg_all[:], scale=-1.0)
        terms = held.tile([P, 1 + PIECES], F32)
        denom = held.tile([P, 1], F32)
        nc.vector.scalar_tensor_tensor(terms[:], rescale[:], 1.0, sums[:], ALU.mult, ALU.mult, accum_out=denom[:])
        inv_denom = held.tile([P, 1], F32)
        nc.vector.reciprocal(inv_denom[:], denom[:])

        partial = held.tile([P, PIECES], F32)
        for c in range(PIECES):
            pv = work.tile([P, PIECE], F32)
            nc.vector.tensor_tensor(pv[:], values[:].indirect(entries(c)), weights[c][:], ALU.mult)
            if c < PIECES - 1:
                copied = work.tile([P, PIECE], BF16)
                nc.scalar.activation(copied[:], pv[:], ACT.Copy, accum_out=partial[:, c : c + 1])
            else:
                nc.vector.tensor_reduce(partial[:, c : c + 1], pv[:], mybir.AxisListType.X, ALU.add)

        scaled = held.tile([P, PIECES], F32)
        nc.vector.scalar_tensor_tensor(
            scaled[:], partial[:], inv_denom[:], rescale[:, 1:], ALU.mult, ALU.mult, accum_out=result[:, 0:1]
        )
        rows = held.tile([P, BLOCK], F32, align_bytes=64)
        nc.vector.transpose(rows[:], result[:])
        nc.sync.dma_start(out.rearrange("o (b j) -> (o b) j", j=BLOCK), rows[0:P:BLOCK, :])
